import numpy as np
import ml_dtypes


def mxq(x, axis, fmt="e4m3"):
    dtype, down = {"e4m3": (ml_dtypes.float8_e4m3fn, 7), "e5m2": (ml_dtypes.float8_e5m2, 14)}[fmt]
    v = np.moveaxis(np.asarray(x, np.float32).astype(ml_dtypes.bfloat16).astype(np.float64), axis, -1)
    blocks = v.reshape(v.shape[:-1] + (-1, 32))
    amax = np.abs(blocks).max(-1, keepdims=True)
    byte = np.maximum(np.where(amax > 0, np.frexp(amax)[1] - 1 + 127, 0) - down, 1)
    scale = np.exp2(byte - 127.0)
    codes = (blocks / scale).astype(np.float32).astype(dtype).astype(np.float64)
    return np.moveaxis((codes * scale).reshape(v.shape), -1, axis)


WIDE = False


def mx_kscale(k):
    if not WIDE:
        return np.ones(k)
    levels = np.array([10, -10, 5, -5, 0])
    if k % 512:
        return np.exp2(np.random.permutation(np.resize(levels, k // 32))).repeat(32)
    a = np.empty((k // 512, 16))
    for p in range(k // 512):
        a[p, :8] = np.random.permutation(np.resize(levels, 8))
        for g in range(8):
            far = levels[np.abs(levels - a[p, g]) >= 10]
            a[p, g + 8] = far[np.random.randint(len(far))]
    return np.exp2(a.ravel()).repeat(32)


BF16 = ml_dtypes.bfloat16


def bf(x):
    return np.asarray(x, np.float32).astype(BF16)


def f64(x):
    return np.asarray(x).astype(np.float64)


E2M1 = np.array([0.0, 0.5, 1.0, 1.5, 2.0, 3.0, 4.0, 6.0, -0.0, -0.5, -1.0, -1.5, -2.0, -3.0, -4.0, -6.0])


def pack_weight(w, fmt):
    k, n = w.shape
    w = f64(bf(w)).reshape(k // 32, 32, n)
    amax = np.abs(w).max(1)
    if fmt == "e4m3":
        byte = np.frexp(amax)[1] - 1 + 127 - 7
    else:
        mant, ex = np.frexp(amax / 6.0)
        byte = np.where(mant > 0.5, ex, ex - 1) + 127
    byte = np.clip(np.where(amax > 0, byte, 1), 1, 254)
    scaled = (w * np.exp2(127.0 - byte)[:, None, :]).reshape(k, n).astype(np.float32)
    by_word = np.ascontiguousarray(scaled.reshape(k // 512, 128, 4, n).transpose(0, 1, 3, 2))
    if fmt == "e4m3":
        words = by_word.astype(ml_dtypes.float8_e4m3fn).view(np.uint8)
    else:
        c = by_word.astype(ml_dtypes.float4_e2m1fn).view(np.uint8) & 0xF
        words = c[..., 0::2] | (c[..., 1::2] << 4)
    return np.ascontiguousarray(words), np.ascontiguousarray(byte.astype(np.uint8).reshape(k // 512, 16, n))


def unpack_weight(words, scales, fmt):
    g, p, n, _ = words.shape
    if fmt == "e4m3":
        vals = np.ascontiguousarray(words).view(ml_dtypes.float8_e4m3fn).astype(np.float64)
    else:
        nib = np.empty((g, p, n, 4), np.uint8)
        nib[..., 0::2] = words & 0xF
        nib[..., 1::2] = words >> 4
        vals = E2M1[nib]
    vals = vals * np.repeat(np.exp2(scales.astype(np.float64) - 127.0), 8, axis=1)[..., None]
    return vals.transpose(0, 1, 3, 2).reshape(g * 512, n)


B, N, E, K, D = 4, 1024, 1024, 256, 1024

EPS = 1e-5


def softmax_last(v):
    e = np.exp(v - np.max(v, axis=-1, keepdims=True))
    return e / np.sum(e, axis=-1, keepdims=True)


def soft_assign(y, w, b):
    logits = (mxq(y, 2, "e4m3") @ w) + b
    return softmax_last(logits)


def rms_intra_norm(v):
    mean_sq = np.mean(v * v, axis=-1, keepdims=True)
    return v / np.sqrt(mean_sq + EPS)


def draw0():
    s, u = mx_kscale(E), mx_kscale(N)
    y = bf(np.random.standard_normal((B, N, E)) * s)
    words, scales = pack_weight(np.random.standard_normal((E, K)) * (1.5 / np.sqrt(E)) / s[:, None], "e4m3")
    return {"y": y,
            "w_words": words,
            "w_scales": scales,
            "b": bf(np.random.standard_normal(K) * 0.5),
            "t": bf(np.random.standard_normal(N) * 0.25 * u),
            "x": bf(np.random.standard_normal((B, N, D)) * (0.016 * K / np.sqrt(N)) / u[:, None]),
            "c": bf(np.random.standard_normal((K, D)) * (0.012 * K / N))}


def core(y, w_words, w_scales, b, t, x, c):
    a = soft_assign(f64(y), unpack_weight(w_words, w_scales, "e4m3"), f64(b))
    r = a * f64(t)[None, :, None]
    rq = mxq(r, 1, "e4m3")
    xq = mxq(f64(x), 1, "e4m3")
    sums = rq.transpose(0, 2, 1) @ xq
    m = np.sum(a, axis=1)
    v = sums - m[:, :, None] * f64(c)[None, :, :]
    return rms_intra_norm(v)


def e4m3fn_bytes(y):
    return np.clip(np.asarray(y, np.float64), -448.0, 448.0).astype(np.float32).astype(ml_dtypes.float8_e4m3fn).view(np.uint8)


def e4m3fn_values(b):
    return np.asarray(b, np.uint8).view(ml_dtypes.float8_e4m3fn).astype(np.float64)


def setup_inputs():
    d = draw0()
    x0 = np.asarray(d['y']).astype(np.float64)
    s = (np.max(np.abs(x0), axis=(0, 1), keepdims=True) / 448.0).astype(np.float32)
    out = {}
    for k, v in d.items():
        if k == 'y':
            out['y_bytes'] = e4m3fn_bytes(x0 / s.astype(np.float64))
            out['y_scale'] = s
        else:
            out[k] = v
    return out


def reference(y_bytes, y_scale, w_words, w_scales, b, t, x, c):
    return core(e4m3fn_values(y_bytes) * y_scale.astype(np.float64), w_words, w_scales, b, t, x, c)

@@ -1,0 +1,348 @@
+from contextlib import ExitStack
+
+import concourse.mybir as mybir
+from concourse.masks import make_identity
+
+B, N, E, K, D = 4, 1024, 1024, 256, 1024
+EPS = 1e-5
+FLOPS = 2 * B * N * E * K + 2 * B * N * K * D
+
+F32 = mybir.dt.float32
+BF16 = mybir.dt.bfloat16
+U32 = mybir.dt.uint32
+I32 = mybir.dt.int32
+U8 = mybir.dt.uint8
+FP8 = mybir.dt.float8_e4m3fn
+FP8X4 = mybir.dt.float8_e4m3fn_x4
+ALU = mybir.AluOpType
+ACT = mybir.ActivationFunctionType
+AXIS = mybir.AxisListType
+
+P = 128
+PACK = 4
+PASS = P * PACK
+GROUPS = B * N // PASS
+HALVES = N // PASS
+E_PASSES = E // PASS
+K_TILES = K // P
+D_TILES = D // PASS
+RUN = 4
+PIECE = D // PACK
+LX = 2
+LE = 2
+XV = ((0, 1),)
+SCV = ((0,1),(1,1),(2,1),(3,1))
+
+
+def tile_crossmodalreweightedvlad_w8_kernel(tc, y_bytes, y_scale, w_words, w_scales, b, t, x, c, out):
+    nc = tc.nc
+    with ExitStack() as ctx:
+        const = ctx.enter_context(tc.tile_pool(name="const", bufs=1))
+        work = ctx.enter_context(tc.tile_pool(name="work", bufs=2))
+        psum = ctx.enter_context(tc.psum_pool(name="psum", bufs=2))
+        ctx.enter_context(tc.manual_schedule(engines={mybir.EngineType.SP}))
+
+        y_raw, x_raw, y_scaled, y_banks, y_grouped, y_codes, y_planes = {}, {}, {}, {}, {}, {}, {}
+        logit_banks, z_by_cluster, z_banks, neg_max, expo, row_sum, inv_sum, coef = {}, {}, {}, {}, {}, {}, {}, {}
+        r_grouped, r_codes, r_planes, x_grouped, x_codes, x_planes = {}, {}, {}, {}, {}, {}
+        mass_banks, mass_rows, neg_mass, sum_banks, resid, squares, mean_sq, rstd, result = {}, {}, {}, {}, {}, {}, {}, {}, {}
+
+        def rows_of(tensor, g):
+            return tensor[g // HALVES, (g % HALVES) * PASS : (g % HALVES + 1) * PASS, :].rearrange("(p j) f -> p j f", j=PACK)
+
+        def load_y(g):
+            y_raw[g] = work.tile([P, PACK, E], U8, name="y_raw", bufs=GROUPS)
+            nc.sync.dma_start(out=y_raw[g][:], in_=rows_of(y_bytes, g))
+
+        def load_x(g, half):
+            x_raw[g, half] = work.tile([P, PACK, PASS], BF16, name="x_raw", bufs=12)
+            nc.sync.dma_start(out=x_raw[g, half][:], in_=rows_of(x, g)[:, :, half * PASS : (half + 1) * PASS])
+
+        ident = const.tile([P, P], F32, name="ident")
+        make_identity(nc, ident[:])
+        minus_half = const.tile([P, 1], F32, name="minus_half")
+        nc.gpsimd.memset(minus_half[:], -0.5)
+        w_plane = const.tile([P, E_PASSES, K], U8, name="w_plane", align_bytes=64)
+        nc.vector.memset(w_plane[:].bitcast(I32), 0)
+        warm = const.tile([P, 1], F32, name="warm")
+        nc.scalar.activation(out=warm[:], in_=minus_half[:], func=ACT.Exp)
+
+        scale_cols = const.tile([P, E // P], F32, name="scale_cols")
+        nc.sync.dma_start(out=scale_cols[:], in_=y_scale.rearrange("o u (p j) -> p (o u j)", p=P))
+        load_x(0, 0)
+        load_y(0)
+        load_x(0, 1)
+        load_y(1)
+        w_code = const.tile([P, E_PASSES, K], U32, name="w_code", align_bytes=64)
+        nc.sync.dma_start(out=w_code[:].bitcast(I32), in_=w_words.rearrange("g p n j -> p g (n j)").bitcast(I32))
+        for quad in range(4):
+            nc.sync.dma_start(
+                out=w_plane[32 * quad : 32 * quad + 4, :, :].bitcast(I32),
+                in_=w_scales[:, 4 * quad : 4 * quad + 4, :].rearrange("g q n -> q g n").bitcast(I32),
+            )
+        bias_raw = const.tile([P, K_TILES, 2], BF16, name="bias_raw")
+        with nc.allow_non_contiguous_dma(reason="one bias value for each partition"):
+            nc.sync.dma_start(out=bias_raw[:, :, 0:1], in_=b.rearrange("(k p o) -> p k o", p=P, o=1))
+        load_x(1, 0)
+        load_x(1, 1)
+        t_cols = const.tile([P, HALVES, PACK], BF16, name="t_cols")
+        nc.sync.dma_start(out=t_cols[:], in_=t.rearrange("(h p j) -> p h j", p=P, j=PACK))
+        for g in range(2, 6):
+            load_y(g)
+            load_x(g, 0)
+            load_x(g, 1)
+        centres = const.tile([P, K_TILES, D], BF16, name="centres")
+        nc.sync.dma_start(out=centres[:], in_=c.rearrange("(k p) d -> p k d", p=P))
+        load_y(6)
+        load_y(7)
+
+        scale_rows = const.tile([P, P, E // P], F32, name="scale_rows")
+
+        def spread_scale(half):
+            bank = psum.tile([P, PACK, P], F32, name="turn_bank")
+            for j in range(PACK):
+                col = half * PACK + j
+                nc.tensor.transpose(bank[:, j, :], scale_cols[:, col : col + 1].to_broadcast([P, P]), ident[:])
+            nc.vector.tensor_copy(out=scale_rows[:, :, half * PACK : (half + 1) * PACK], in_=bank[:].rearrange("q j n -> q n j"))
+
+        def scale_y(g, j):
+            y_scaled[g, j] = work.tile([P, E], BF16, name="y_scaled", bufs=4)
+            nc.vector.tensor_tensor(
+                out=y_scaled[g, j][:], in0=y_raw[g][:, j, :].bitcast(FP8), in1=scale_rows[:].rearrange("q n j -> q (n j)"), op=ALU.mult
+            )
+
+        def turn_y(g, j):
+            words = y_scaled[g, j][:].bitcast(F32)
+            y_banks[g, j] = psum.tile([P, E_PASSES, 2, P], F32, name="turn_bank")
+            for a in range(E_PASSES):
+                for u in range(2):
+                    nc.tensor.transpose(y_banks[g, j][:, a, u, :], words[:, 2 * P * a + u : 2 * P * (a + 1) : 2], ident[:])
+
+        def group_y(g, j):
+            if j == 0:
+                y_grouped[g] = work.tile([P, E_PASSES, PACK, P, 2], F32, name="y_grouped", align_bytes=64)
+            nc.scalar.copy(out=y_grouped[g][:, :, j, :, :], in_=y_banks[g, j][:].rearrange("q a u p -> q a p u"))
+
+        def quantize_y(g):
+            y_codes[g] = work.tile([P, E_PASSES * PASS], U32, name="y_codes", align_bytes=64)
+            y_planes[g] = work.tile([P, E_PASSES * PASS], U8, name="y_planes", align_bytes=64)
+            nc.vector.quantize_mx(
+                out=y_codes[g][:].bitcast(FP8X4),
+                scales=y_planes[g][:],
+                in_=y_grouped[g][:].rearrange("q a j p u -> q (a j p u)").bitcast(BF16),
+            )
+
+        def logits(g, k):
+            logit_banks[g, k] = psum.tile([P, PASS], F32, name="logit_bank", bufs=1)
+            for a in range(E_PASSES):
+                nc.tensor.matmul_mx(
+                    out=logit_banks[g, k][:],
+                    lhsT=w_code[:, a, k * P : (k + 1) * P].bitcast(FP8X4),
+                    lhsT_scale=w_plane[:, a, k * P : (k + 1) * P],
+                    rhs=y_codes[g][:, a * PASS : (a + 1) * PASS].bitcast(FP8X4),
+                    rhs_scale=y_planes[g][:, a * PASS : (a + 1) * PASS],
+                    start=(a == 0),
+                    stop=(a == E_PASSES - 1),
+                )
+
+        def add_bias(g, k):
+            z_by_cluster[g, k] = work.tile([P, PASS], F32, name="z_by_cluster", bufs=3)
+            nc.scalar.activation(
+                out=z_by_cluster[g, k][:], in_=logit_banks[g, k][:], func=ACT.Identity, bias=bias_raw[:, k, 0:1]
+            )
+
+        def turn_z(g, pair):
+            z_banks[g, pair] = psum.tile([P, 2, K], F32, name="z_bank")
+            for jj in range(2):
+                j = 2 * pair + jj
+                for k in range(K_TILES):
+                    nc.tensor.transpose(z_banks[g, pair][:, jj, k * P : (k + 1) * P], z_by_cluster[g, k][:, j * P : (j + 1) * P], ident[:])
+
+        def find_max(g, pair):
+            neg_max[g, pair] = work.tile([P, 2], F32, name="neg_max", bufs=4)
+            nc.vector.tensor_reduce(out=neg_max[g, pair][:], in_=z_banks[g, pair][:], axis=AXIS.X, op=ALU.max, negate=True)
+
+        def exponentiate(g, j):
+            if j == 0:
+                expo[g] = work.tile([P, PACK, K], F32, name="expo", bufs=3)
+                row_sum[g] = work.tile([P, PACK], F32, name="row_sum")
+            nc.scalar.activation(
+                out=expo[g][:, j, :],
+                in_=z_banks[g, j // 2][:, j % 2, :],
+                func=ACT.Exp,
+                bias=neg_max[g, j // 2][:, j % 2 : j % 2 + 1],
+                accum_out=row_sum[g][:, j : j + 1],
+            )
+
+        def invert_sum(g):
+            inv_sum[g] = work.tile([P, PACK], F32, name="inv_sum")
+            nc.vector.reciprocal(out=inv_sum[g][:], in_=row_sum[g][:])
+
+        def make_coef(g):
+            coef[g] = work.tile([P, PACK], F32, name="coef")
+            nc.vector.tensor_tensor(out=coef[g][:], in0=inv_sum[g][:], in1=t_cols[:, g % HALVES, :], op=ALU.mult)
+
+        def reweight(g):
+            r_grouped[g] = work.tile([P, K, PACK], BF16, name="r_grouped", align_bytes=64)
+            nc.vector.tensor_tensor(
+                out=r_grouped[g][:].rearrange("p (c i) j -> p c j i", i=RUN),
+                in0=expo[g][:].rearrange("p j (c i) -> p c j i", i=RUN),
+                in1=coef[g][:].unsqueeze(1).unsqueeze(3).to_broadcast([P, K // RUN, PACK, RUN]),
+                op=ALU.mult,
+            )
+
+        def quantize_r(g):
+            r_codes[g] = work.tile([P, K], U32, name="r_codes", bufs=6, align_bytes=64)
+            r_planes[g] = work.tile([P, K], U8, name="r_planes", bufs=6, align_bytes=64)
+            nc.vector.quantize_mx(
+                out=r_codes[g][:].bitcast(FP8X4), scales=r_planes[g][:], in_=r_grouped[g][:].rearrange("p k j -> p (k j)")
+            )
+
+        def add_mass(g, j):
+            i = g // HALVES
+            first = g % HALVES == 0 and j == 0
+            if first:
+                mass_banks[i] = psum.tile([P, 2, K], F32, name="mass_bank", bufs=1)
+            nc.tensor.matmul(
+                out=mass_banks[i][:, 0, :],
+                lhsT=inv_sum[g][:, j : j + 1].to_broadcast([P, P]),
+                rhs=expo[g][:, j, :],
+                start=first,
+                stop=(g % HALVES == HALVES - 1 and j == PACK - 1),
+            )
+
+        def copy_mass(i):
+            mass_rows[i] = work.tile([P, K], F32, name="mass_rows")
+            nc.scalar.copy(out=mass_rows[i][:], in_=mass_banks[i][:, 0, :])
+
+        def turn_mass(i):
+            for k in range(K_TILES):
+                nc.tensor.transpose(mass_banks[i][:, 1, k * P : (k + 1) * P], mass_rows[i][:, k * P : (k + 1) * P], ident[:])
+
+        def negate_mass(i):
+            neg_mass[i] = work.tile([P, K_TILES], F32, name="neg_mass", bufs=4)
+            nc.scalar.activation(out=neg_mass[i][:], in_=mass_banks[i][:, 1, 0:K:P], func=ACT.Copy, scale=-1.0)
+
+        def group_x(g, piece, on_vector):
+            if piece == 0:
+                x_grouped[g] = work.tile([P, D, PACK], BF16, name="x_grouped", bufs=3, align_bytes=64)
+            src = x_raw[g, piece // 2][:, :, (piece % 2) * PIECE : (piece % 2 + 1) * PIECE].rearrange("p j (c i) -> p c j i", i=RUN)
+            dst = x_grouped[g][:, piece * PIECE : (piece + 1) * PIECE, :].rearrange("p (c i) j -> p c j i", i=RUN)
+            if on_vector:
+                nc.vector.tensor_copy(out=dst, in_=src)
+            else:
+                nc.scalar.copy(out=dst, in_=src)
+
+        def quantize_x(g):
+            x_codes[g] = work.tile([P, D], U32, name="x_codes", bufs=4, align_bytes=64)
+            x_planes[g] = work.tile([P, D], U8, name="x_planes", bufs=4, align_bytes=64)
+            nc.vector.quantize_mx(
+                out=x_codes[g][:].bitcast(FP8X4), scales=x_planes[g][:], in_=x_grouped[g][:].rearrange("p d j -> p (d j)")
+            )
+
+        def weighted_sums(i, k, dt):
+            sum_banks[i, k, dt] = psum.tile([P, PASS], F32, name="sum_bank")
+            for h in range(HALVES):
+                g = i * HALVES + h
+                nc.tensor.matmul_mx(
+                    out=sum_banks[i, k, dt][:],
+                    lhsT=r_codes[g][:, k * P : (k + 1) * P].bitcast(FP8X4),
+                    lhsT_scale=r_planes[g][:, k * P : (k + 1) * P],
+                    rhs=x_codes[g][:, dt * PASS : (dt + 1) * PASS].bitcast(FP8X4),
+                    rhs_scale=x_planes[g][:, dt * PASS : (dt + 1) * PASS],
+                    start=(h == 0),
+                    stop=(h == HALVES - 1),
+                )
+
+        def subtract_centres(i, k, dt):
+            if dt == 0:
+                resid[i, k] = work.tile([P, D], F32, name="resid", bufs=4)
+            cols = slice(dt * PASS, (dt + 1) * PASS)
+            nc.vector.scalar_tensor_tensor(
+                out=resid[i, k][:, cols],
+                in0=centres[:, k, cols],
+                scalar=neg_mass[i][:, k : k + 1],
+                in1=sum_banks[i, k, dt][:],
+                op0=ALU.mult,
+                op1=ALU.add,
+            )
+
+        def sum_squares(i, k, dt):
+            if dt == 0:
+                squares[i, k] = work.tile([P, D_TILES], F32, name="squares", bufs=4)
+                result[i, k] = work.tile([P, D], F32, name="result", bufs=4)
+            cols = slice(dt * PASS, (dt + 1) * PASS)
+            nc.scalar.activation(
+                out=result[i, k][:, cols],
+                in_=resid[i, k][:, cols],
+                func=ACT.Square,
+                scale=D**-0.5,
+                accum_out=squares[i, k][:, dt : dt + 1],
+            )
+
+        def add_eps(i, k):
+            mean_sq[i, k] = work.tile([P, 1], F32, name="mean_sq", bufs=4)
+            nc.vector.tensor_scalar(
+                out=mean_sq[i, k][:], in0=squares[i, k][:, 0:1], scalar1=squares[i, k][:, 1:2], scalar2=EPS, op0=ALU.add, op1=ALU.add
+            )
+            rstd[i, k] = work.tile([P, 1], F32, name="rstd", bufs=4)
+            nc.gpsimd.tensor_tensor(out=rstd[i, k][:], in0=mean_sq[i, k][:], in1=minus_half[:], op=ALU.pow)
+
+        def normalise(i, k, on_vector):
+            if on_vector:
+                nc.vector.tensor_scalar(out=result[i, k][:], in0=resid[i, k][:], scalar1=rstd[i, k][:], scalar2=None, op0=ALU.mult)
+            else:
+                nc.scalar.activation(out=result[i, k][:], in_=resid[i, k][:], func=ACT.Copy, scale=rstd[i, k][:])
+            nc.sync.dma_start(out=out[i, k * P : (k + 1) * P, :], in_=result[i, k][:])
+
+        def when(ok, stage, *args):
+            if ok:
+                stage(*args)
+
+        spread_scale(0)
+        spread_scale(1)
+
+        def assign(g):
+            for j in range(PACK):
+                scale_y(g, j)
+                turn_y(g, j)
+                group_y(g, j)
+            quantize_y(g)
+            for k in range(K_TILES):
+                logits(g, k)
+                add_bias(g, k)
+            for pair in range(2):
+                turn_z(g, pair)
+                find_max(g, pair)
+                exponentiate(g, 2 * pair)
+                exponentiate(g, 2 * pair + 1)
+            invert_sum(g)
+            make_coef(g)
+            reweight(g)
+            quantize_r(g)
+            for j in range(PACK):
+                add_mass(g, j)
+            if g % HALVES == HALVES - 1:
+                copy_mass(g // HALVES)
+                turn_mass(g // HALVES)
+                negate_mass(g // HALVES)
+
+        def prepare_x(g):
+            for piece in range(PACK):
+                group_x(g, piece, (g, piece) in XV)
+            quantize_x(g)
+            when(g + 6 < GROUPS, load_x, g + 6, 0)
+            when(g + 6 < GROUPS, load_x, g + 6, 1)
+
+        def pool(i, k):
+            for dt in range(D_TILES):
+                weighted_sums(i, k, dt)
+                subtract_centres(i, k, dt)
+                sum_squares(i, k, dt)
+            add_eps(i, k)
+            normalise(i, k, (i, k) in SCV)
+
+        for step in range(GROUPS + LE + 2):
+            when(step < GROUPS, assign, step)
+            when(0 <= step - LX < GROUPS, prepare_x, step - LX)
+            when(0 <= step - LE - 1 < GROUPS, pool, *divmod(step - LE - 1, K_TILES))

@@ -29,7 +29,7 @@ D_TILES = D // PASS
 RUN = 4
 PIECE = D // PACK
 LX = 2
-LE = 2
+LE = 3
 XV = ((0, 1),)
 SCV = ((0,1),(1,1),(2,1),(3,1))
 
@@ -185,9 +185,9 @@ def tile_crossmodalreweightedvlad_w8_kernel(tc, y_bytes, y_scale, w_words, w_sca
         def reweight(g):
             r_grouped[g] = work.tile([P, K, PACK], BF16, name="r_grouped", align_bytes=64)
             nc.vector.tensor_tensor(
-                out=r_grouped[g][:].rearrange("p (c i) j -> p c j i", i=RUN),
-                in0=expo[g][:].rearrange("p j (c i) -> p c j i", i=RUN),
-                in1=coef[g][:].unsqueeze(1).unsqueeze(3).to_broadcast([P, K // RUN, PACK, RUN]),
+                out=r_grouped[g][:].rearrange("p (c i) j -> p c j i", i=2),
+                in0=expo[g][:].rearrange("p j (c i) -> p c j i", i=2),
+                in1=coef[g][:].unsqueeze(1).unsqueeze(3).to_broadcast([P, K // 2, PACK, 2]),
                 op=ALU.mult,
             )
 

@@ -27,11 +27,9 @@ E_PASSES = E // PASS
 K_TILES = K // P
 D_TILES = D // PASS
 RUN = 4
+X_AHEAD = 5
 PIECE = D // PACK
-LX = 2
-LE = 3
-XV = ((0, 1),)
-SCV = ((0,1),(1,1),(2,1),(3,1))
+XN = (3, 3, 3, 3, 3, 3, 3, 3)
 
 
 def tile_crossmodalreweightedvlad_w8_kernel(tc, y_bytes, y_scale, w_words, w_scales, b, t, x, c, out):
@@ -40,7 +38,7 @@ def tile_crossmodalreweightedvlad_w8_kernel(tc, y_bytes, y_scale, w_words, w_sca
         const = ctx.enter_context(tc.tile_pool(name="const", bufs=1))
         work = ctx.enter_context(tc.tile_pool(name="work", bufs=2))
         psum = ctx.enter_context(tc.psum_pool(name="psum", bufs=2))
-        ctx.enter_context(tc.manual_schedule(engines={mybir.EngineType.SP}))
+        ctx.enter_context(tc.manual_schedule())
 
         y_raw, x_raw, y_scaled, y_banks, y_grouped, y_codes, y_planes = {}, {}, {}, {}, {}, {}, {}
         logit_banks, z_by_cluster, z_banks, neg_max, expo, row_sum, inv_sum, coef = {}, {}, {}, {}, {}, {}, {}, {}
@@ -55,7 +53,7 @@ def tile_crossmodalreweightedvlad_w8_kernel(tc, y_bytes, y_scale, w_words, w_sca
             nc.sync.dma_start(out=y_raw[g][:], in_=rows_of(y_bytes, g))
 
         def load_x(g, half):
-            x_raw[g, half] = work.tile([P, PACK, PASS], BF16, name="x_raw", bufs=12)
+            x_raw[g, half] = work.tile([P, PACK, PASS], BF16, name="x_raw", bufs=2 * X_AHEAD)
             nc.sync.dma_start(out=x_raw[g, half][:], in_=rows_of(x, g)[:, :, half * PASS : (half + 1) * PASS])
 
         ident = const.tile([P, P], F32, name="ident")
@@ -87,14 +85,14 @@ def tile_crossmodalreweightedvlad_w8_kernel(tc, y_bytes, y_scale, w_words, w_sca
         load_x(1, 1)
         t_cols = const.tile([P, HALVES, PACK], BF16, name="t_cols")
         nc.sync.dma_start(out=t_cols[:], in_=t.rearrange("(h p j) -> p h j", p=P, j=PACK))
-        for g in range(2, 6):
+        for g in range(2, X_AHEAD):
             load_y(g)
             load_x(g, 0)
             load_x(g, 1)
         centres = const.tile([P, K_TILES, D], BF16, name="centres")
         nc.sync.dma_start(out=centres[:], in_=c.rearrange("(k p) d -> p k d", p=P))
-        load_y(6)
-        load_y(7)
+        for g in range(X_AHEAD, GROUPS):
+            load_y(g)
 
         scale_rows = const.tile([P, P, E // P], F32, name="scale_rows")
 
@@ -232,16 +230,18 @@ def tile_crossmodalreweightedvlad_w8_kernel(tc, y_bytes, y_scale, w_words, w_sca
                 nc.vector.tensor_copy(out=dst, in_=src)
             else:
                 nc.scalar.copy(out=dst, in_=src)
+            if piece % 2 == 1 and g + X_AHEAD < GROUPS:
+                load_x(g + X_AHEAD, piece // 2)
 
         def quantize_x(g):
-            x_codes[g] = work.tile([P, D], U32, name="x_codes", bufs=4, align_bytes=64)
-            x_planes[g] = work.tile([P, D], U8, name="x_planes", bufs=4, align_bytes=64)
+            x_codes[g] = work.tile([P, D], U32, name="x_codes", bufs=5, align_bytes=64)
+            x_planes[g] = work.tile([P, D], U8, name="x_planes", bufs=5, align_bytes=64)
             nc.vector.quantize_mx(
                 out=x_codes[g][:].bitcast(FP8X4), scales=x_planes[g][:], in_=x_grouped[g][:].rearrange("p d j -> p (d j)")
             )
 
-        def weighted_sums(i, k, dt):
-            sum_banks[i, k, dt] = psum.tile([P, PASS], F32, name="sum_bank")
+        def weighted_sums(i, k, dt, bank_name="sum_bank"):
+            sum_banks[i, k, dt] = psum.tile([P, PASS], F32, name=bank_name)
             for h in range(HALVES):
                 g = i * HALVES + h
                 nc.tensor.matmul_mx(
@@ -288,61 +288,166 @@ def tile_crossmodalreweightedvlad_w8_kernel(tc, y_bytes, y_scale, w_words, w_sca
             rstd[i, k] = work.tile([P, 1], F32, name="rstd", bufs=4)
             nc.gpsimd.tensor_tensor(out=rstd[i, k][:], in0=mean_sq[i, k][:], in1=minus_half[:], op=ALU.pow)
 
-        def normalise(i, k, on_vector):
+        def normalise(i, k, on_vector, cols=slice(0, D)):
             if on_vector:
-                nc.vector.tensor_scalar(out=result[i, k][:], in0=resid[i, k][:], scalar1=rstd[i, k][:], scalar2=None, op0=ALU.mult)
+                nc.vector.tensor_scalar(out=result[i, k][:, cols], in0=resid[i, k][:, cols], scalar1=rstd[i, k][:], scalar2=None, op0=ALU.mult)
             else:
-                nc.scalar.activation(out=result[i, k][:], in_=resid[i, k][:], func=ACT.Copy, scale=rstd[i, k][:])
-            nc.sync.dma_start(out=out[i, k * P : (k + 1) * P, :], in_=result[i, k][:])
+                nc.scalar.activation(out=result[i, k][:, cols], in_=resid[i, k][:, cols], func=ACT.Copy, scale=rstd[i, k][:])
+            nc.sync.dma_start(out=out[i, k * P : (k + 1) * P, cols], in_=result[i, k][:, cols])
 
         def when(ok, stage, *args):
             if ok:
                 stage(*args)
 
+        group_x(0, 0, False)
         spread_scale(0)
+        group_x(0, 1, True)
         spread_scale(1)
+        scale_y(0, 0)
+        turn_y(0, 0)
+        group_x(0, 2, False)
+        group_x(0, 3, False)
 
-        def assign(g):
+        pieces = [(g, piece) for g in range(1, GROUPS) for piece in range(PACK)]
+        slots = [(step, q) for step in range(GROUPS) for q in range(XN[step])]
+        x_slot = dict(zip(slots, pieces))
+        x_ready = {step + (q > 0): g for (step, q), (g, piece) in x_slot.items() if piece == PACK - 1}
+        x_ready[0] = 0
+
+        def x_piece(step, q):
+            if (step, q) in x_slot:
+                group_x(*x_slot[step, q], False)
+
+        for step in range(GROUPS):
+            ga, gb, gc, gd = step, step - 1, step - 2, step - 3
+            n_on, b_on, c_on, d_on = step + 1 < GROUPS, gb >= 0, gc >= 0, gd >= 0
+            ip, kp = divmod(step - 4, K_TILES)
+            p_on = ip >= 0
+            io, ko = divmod(step - 5, K_TILES)
+            o_on = io >= 0
+            m_on = d_on and gd % HALVES == HALVES - 1
+
+            scale_y(ga, 1)
+            when(c_on, find_max, gc, 0)
+            when(d_on, quantize_r, gd)
+            when(c_on, find_max, gc, 1)
+            when(d_on, add_mass, gd, 2)
+            when(d_on, add_mass, gd, 3)
+            turn_y(ga, 1)
+            group_y(ga, 0)
+            when(o_on, sum_squares, io, ko, 1)
+            x_piece(step, 0)
+            when(m_on, copy_mass, gd // HALVES)
+
+            when(b_on, quantize_y, gb)
+            scale_y(ga, 2)
+            when(p_on, weighted_sums, ip, kp, 0)
+            when(m_on, turn_mass, gd // HALVES)
+            when(b_on, logits, gb, 0)
+            turn_y(ga, 2)
             for j in range(PACK):
-                scale_y(g, j)
-                turn_y(g, j)
-                group_y(g, j)
-            quantize_y(g)
-            for k in range(K_TILES):
-                logits(g, k)
-                add_bias(g, k)
-            for pair in range(2):
-                turn_z(g, pair)
-                find_max(g, pair)
-                exponentiate(g, 2 * pair)
-                exponentiate(g, 2 * pair + 1)
-            invert_sum(g)
-            make_coef(g)
-            reweight(g)
-            quantize_r(g)
-            for j in range(PACK):
-                add_mass(g, j)
-            if g % HALVES == HALVES - 1:
-                copy_mass(g // HALVES)
-                turn_mass(g // HALVES)
-                negate_mass(g // HALVES)
+                when(c_on, exponentiate, gc, j)
+            when(m_on, negate_mass, gd // HALVES)
+            group_y(ga, 1)
+            when(b_on, add_bias, gb, 0)
 
-        def prepare_x(g):
-            for piece in range(PACK):
-                group_x(g, piece, (g, piece) in XV)
-            quantize_x(g)
-            when(g + 6 < GROUPS, load_x, g + 6, 0)
-            when(g + 6 < GROUPS, load_x, g + 6, 1)
+            scale_y(ga, 3)
+            when(o_on, add_eps, io, ko)
+            when(p_on, subtract_centres, ip, kp, 0)
+            when(c_on, invert_sum, gc)
+            when(step in x_ready, quantize_x, x_ready.get(step))
+            when(p_on, weighted_sums, ip, kp, 1)
+            when(b_on, logits, gb, 1)
+            turn_y(ga, 3)
+            x_piece(step, 1)
+            when(b_on, add_bias, gb, 1)
+            group_y(ga, 2)
 
-        def pool(i, k):
+            when(c_on, make_coef, gc)
+            when(n_on, scale_y, ga + 1, 0)
+            when(c_on, reweight, gc)
+            when(p_on, subtract_centres, ip, kp, 1)
+            when(o_on, normalise, io, ko, True)
+            when(c_on, add_mass, gc, 0)
+            when(b_on, turn_z, gb, 0)
+            when(b_on, turn_z, gb, 1)
+            when(c_on, add_mass, gc, 1)
+            group_y(ga, 3)
+            when(n_on, turn_y, ga + 1, 0)
+            when(p_on, sum_squares, ip, kp, 0)
+            x_piece(step, 2)
+            x_piece(step, 3)
+
+        quantize_y(7)
+        find_max(6, 0)
+        quantize_r(5)
+        find_max(6, 1)
+        quantize_x(6)
+        add_mass(5, 2)
+        add_mass(5, 3)
+        logits(7, 0)
+        sum_squares(1, 1, 1)
+        copy_mass(2)
+        group_x(7, 0, False)
+        add_bias(7, 0)
+        turn_mass(2)
+        logits(7, 1)
+        weighted_sums(2, 0, 0)
+        weighted_sums(2, 0, 1)
+        for j in range(PACK):
+            exponentiate(6, j)
+        negate_mass(2)
+        add_bias(7, 1)
+        invert_sum(6)
+        add_eps(1, 1)
+        subtract_centres(2, 0, 0)
+        make_coef(6)
+        subtract_centres(2, 0, 1)
+        turn_z(7, 0)
+        turn_z(7, 1)
+        weighted_sums(2, 1, 0)
+        weighted_sums(2, 1, 1)
+        for j in range(PACK):
+            add_mass(6, j)
+        group_x(7, 1, False)
+        sum_squares(2, 0, 0)
+        sum_squares(2, 0, 1)
+        reweight(6)
+        find_max(7, 0)
+        find_max(7, 1)
+        for j in range(PACK):
+            exponentiate(7, j)
+        normalise(1, 1, True)
+        quantize_r(6)
+        add_eps(2, 0)
+        subtract_centres(2, 1, 0)
+        subtract_centres(2, 1, 1)
+        invert_sum(7)
+        group_x(7, 2, False)
+        make_coef(7)
+        for j in range(PACK):
+            add_mass(7, j)
+        group_x(7, 3, False)
+        normalise(2, 0, True)
+        reweight(7)
+        quantize_x(7)
+        quantize_r(7)
+        sum_squares(2, 1, 0)
+        copy_mass(3)
+        turn_mass(3)
+        sum_squares(2, 1, 1)
+        negate_mass(3)
+        add_eps(2, 1)
+        for k in range(K_TILES):
             for dt in range(D_TILES):
-                weighted_sums(i, k, dt)
-                subtract_centres(i, k, dt)
-                sum_squares(i, k, dt)
-            add_eps(i, k)
-            normalise(i, k, (i, k) in SCV)
-
-        for step in range(GROUPS + LE + 2):
-            when(step < GROUPS, assign, step)
-            when(0 <= step - LX < GROUPS, prepare_x, step - LX)
-            when(0 <= step - LE - 1 < GROUPS, pool, *divmod(step - LE - 1, K_TILES))
+                weighted_sums(3, k, dt, "turn_bank" if k else "sum_bank")
+        for k in range(K_TILES):
+            for dt in range(D_TILES):
+                subtract_centres(3, k, dt)
+                when(k + dt == 0, normalise, 2, 1, False)
+                when(k + dt == 2, add_eps, 3, 0)
+                sum_squares(3, k, dt)
+        normalise(3, 0, True)
+        add_eps(3, 1)
+        for dt in range(D_TILES):
+            normalise(3, 1, True, slice(dt * PASS, (dt + 1) * PASS))

@@ -30,6 +30,7 @@ RUN = 4
 X_AHEAD = 5
 PIECE = D // PACK
 XN = (3, 3, 3, 3, 3, 3, 3, 3)
+SV = (7,)
 
 
 def tile_crossmodalreweightedvlad_w8_kernel(tc, y_bytes, y_scale, w_words, w_scales, b, t, x, c, out):
@@ -42,6 +43,7 @@ def tile_crossmodalreweightedvlad_w8_kernel(tc, y_bytes, y_scale, w_words, w_sca
 
         y_raw, x_raw, y_scaled, y_banks, y_grouped, y_codes, y_planes = {}, {}, {}, {}, {}, {}, {}
         logit_banks, z_by_cluster, z_banks, neg_max, expo, row_sum, inv_sum, coef = {}, {}, {}, {}, {}, {}, {}, {}
+        x_banks = {}
         r_grouped, r_codes, r_planes, x_grouped, x_codes, x_planes = {}, {}, {}, {}, {}, {}
         mass_banks, mass_rows, neg_mass, sum_banks, resid, squares, mean_sq, rstd, result = {}, {}, {}, {}, {}, {}, {}, {}, {}
 
@@ -60,6 +62,8 @@ def tile_crossmodalreweightedvlad_w8_kernel(tc, y_bytes, y_scale, w_words, w_sca
         make_identity(nc, ident[:])
         minus_half = const.tile([P, 1], F32, name="minus_half")
         nc.gpsimd.memset(minus_half[:], -0.5)
+        ident_bf16 = const.tile([P, P], BF16, name="ident_bf16")
+        make_identity(nc, ident_bf16[:])
         w_plane = const.tile([P, E_PASSES, K], U8, name="w_plane", align_bytes=64)
         nc.vector.memset(w_plane[:].bitcast(I32), 0)
         warm = const.tile([P, 1], F32, name="warm")
@@ -70,6 +74,7 @@ def tile_crossmodalreweightedvlad_w8_kernel(tc, y_bytes, y_scale, w_words, w_sca
         load_x(0, 0)
         load_y(0)
         load_x(0, 1)
+        load_x(1, 0)
         load_y(1)
         w_code = const.tile([P, E_PASSES, K], U32, name="w_code", align_bytes=64)
         nc.sync.dma_start(out=w_code[:].bitcast(I32), in_=w_words.rearrange("g p n j -> p g (n j)").bitcast(I32))
@@ -81,7 +86,6 @@ def tile_crossmodalreweightedvlad_w8_kernel(tc, y_bytes, y_scale, w_words, w_sca
         bias_raw = const.tile([P, K_TILES, 2], BF16, name="bias_raw")
         with nc.allow_non_contiguous_dma(reason="one bias value for each partition"):
             nc.sync.dma_start(out=bias_raw[:, :, 0:1], in_=b.rearrange("(k p o) -> p k o", p=P, o=1))
-        load_x(1, 0)
         load_x(1, 1)
         t_cols = const.tile([P, HALVES, PACK], BF16, name="t_cols")
         nc.sync.dma_start(out=t_cols[:], in_=t.rearrange("(h p j) -> p h j", p=P, j=PACK))
@@ -221,17 +225,34 @@ def tile_crossmodalreweightedvlad_w8_kernel(tc, y_bytes, y_scale, w_words, w_sca
             neg_mass[i] = work.tile([P, K_TILES], F32, name="neg_mass", bufs=4)
             nc.scalar.activation(out=neg_mass[i][:], in_=mass_banks[i][:, 1, 0:K:P], func=ACT.Copy, scale=-1.0)
 
-        def group_x(g, piece, on_vector):
+        def group_x(g, piece):
             if piece == 0:
                 x_grouped[g] = work.tile([P, D, PACK], BF16, name="x_grouped", bufs=3, align_bytes=64)
             src = x_raw[g, piece // 2][:, :, (piece % 2) * PIECE : (piece % 2 + 1) * PIECE].rearrange("p j (c i) -> p c j i", i=RUN)
             dst = x_grouped[g][:, piece * PIECE : (piece + 1) * PIECE, :].rearrange("p (c i) j -> p c j i", i=RUN)
-            if on_vector:
-                nc.vector.tensor_copy(out=dst, in_=src)
-            else:
-                nc.scalar.copy(out=dst, in_=src)
+            nc.scalar.copy(out=dst, in_=src)
             if piece % 2 == 1 and g + X_AHEAD < GROUPS:
                 load_x(g + X_AHEAD, piece // 2)
+
+        def weave_x(g, piece):
+            x_banks[g, piece] = psum.tile([P, 2, PASS], BF16, name="turn_bank")
+            for half in range(2):
+                first = (piece % 2) * PIECE + half * P
+                nc.tensor.matmul(
+                    out=x_banks[g, piece][:, half, :],
+                    lhsT=ident_bf16[:],
+                    rhs=x_raw[g, piece // 2][:, :, first : first + P].rearrange("p j d -> p d j"),
+                    start=True,
+                    stop=True,
+                )
+
+        def copy_woven_x(g, piece):
+            if piece == 0:
+                x_grouped[g] = work.tile([P, D, PACK], BF16, name="x_grouped", bufs=3, align_bytes=64)
+            nc.scalar.copy(
+                out=x_grouped[g][:, piece * PIECE : (piece + 1) * PIECE, :].rearrange("p d j -> p (d j)"),
+                in_=x_banks[g, piece][:].rearrange("p h n -> p (h n)"),
+            )
 
         def quantize_x(g):
             x_codes[g] = work.tile([P, D], U32, name="x_codes", bufs=5, align_bytes=64)
@@ -299,14 +320,13 @@ def tile_crossmodalreweightedvlad_w8_kernel(tc, y_bytes, y_scale, w_words, w_sca
             if ok:
                 stage(*args)
 
-        group_x(0, 0, False)
+        group_x(0, 0)
         spread_scale(0)
-        group_x(0, 1, True)
         spread_scale(1)
         scale_y(0, 0)
         turn_y(0, 0)
-        group_x(0, 2, False)
-        group_x(0, 3, False)
+        for piece in range(1, PACK):
+            group_x(0, piece)
 
         pieces = [(g, piece) for g in range(1, GROUPS) for piece in range(PACK)]
         slots = [(step, q) for step in range(GROUPS) for q in range(XN[step])]
@@ -316,7 +336,7 @@ def tile_crossmodalreweightedvlad_w8_kernel(tc, y_bytes, y_scale, w_words, w_sca
 
         def x_piece(step, q):
             if (step, q) in x_slot:
-                group_x(*x_slot[step, q], False)
+                group_x(*x_slot[step, q])
 
         for step in range(GROUPS):
             ga, gb, gc, gd = step, step - 1, step - 2, step - 3
@@ -367,39 +387,46 @@ def tile_crossmodalreweightedvlad_w8_kernel(tc, y_bytes, y_scale, w_words, w_sca
             when(n_on, scale_y, ga + 1, 0)
             when(c_on, reweight, gc)
             when(p_on, subtract_centres, ip, kp, 1)
-            when(o_on, normalise, io, ko, True)
+            when(o_on and step in SV, normalise, io, ko, True)
             when(c_on, add_mass, gc, 0)
             when(b_on, turn_z, gb, 0)
             when(b_on, turn_z, gb, 1)
             when(c_on, add_mass, gc, 1)
             group_y(ga, 3)
             when(n_on, turn_y, ga + 1, 0)
+            when(not n_on, weave_x, ga, 0)
             when(p_on, sum_squares, ip, kp, 0)
             x_piece(step, 2)
-            x_piece(step, 3)
+            when(o_on and step not in SV, normalise, io, ko, False)
 
         quantize_y(7)
+        sum_squares(1, 1, 1)
+        add_eps(1, 1)
         find_max(6, 0)
-        quantize_r(5)
         find_max(6, 1)
+        quantize_r(5)
         quantize_x(6)
+        normalise(1, 1, True)
         add_mass(5, 2)
         add_mass(5, 3)
-        logits(7, 0)
-        sum_squares(1, 1, 1)
+        weave_x(7, 1)
+        copy_woven_x(7, 0)
         copy_mass(2)
-        group_x(7, 0, False)
+        logits(7, 0)
+        copy_woven_x(7, 1)
         add_bias(7, 0)
         turn_mass(2)
+        weave_x(7, 2)
         logits(7, 1)
         weighted_sums(2, 0, 0)
         weighted_sums(2, 0, 1)
         for j in range(PACK):
             exponentiate(6, j)
         negate_mass(2)
+        weave_x(7, 3)
         add_bias(7, 1)
+        copy_woven_x(7, 2)
         invert_sum(6)
-        add_eps(1, 1)
         subtract_centres(2, 0, 0)
         make_coef(6)
         subtract_centres(2, 0, 1)
@@ -409,42 +436,39 @@ def tile_crossmodalreweightedvlad_w8_kernel(tc, y_bytes, y_scale, w_words, w_sca
         weighted_sums(2, 1, 1)
         for j in range(PACK):
             add_mass(6, j)
-        group_x(7, 1, False)
         sum_squares(2, 0, 0)
         sum_squares(2, 0, 1)
-        reweight(6)
         find_max(7, 0)
         find_max(7, 1)
         for j in range(PACK):
             exponentiate(7, j)
-        normalise(1, 1, True)
-        quantize_r(6)
+        copy_woven_x(7, 3)
         add_eps(2, 0)
         subtract_centres(2, 1, 0)
         subtract_centres(2, 1, 1)
         invert_sum(7)
-        group_x(7, 2, False)
+        reweight(6)
         make_coef(7)
         for j in range(PACK):
             add_mass(7, j)
-        group_x(7, 3, False)
-        normalise(2, 0, True)
-        reweight(7)
-        quantize_x(7)
-        quantize_r(7)
         sum_squares(2, 1, 0)
+        sum_squares(2, 1, 1)
+        normalise(2, 0, False)
+        quantize_x(7)
+        quantize_r(6)
+        reweight(7)
+        add_eps(2, 1)
+        quantize_r(7)
         copy_mass(3)
         turn_mass(3)
-        sum_squares(2, 1, 1)
         negate_mass(3)
-        add_eps(2, 1)
+        normalise(2, 1, True)
         for k in range(K_TILES):
             for dt in range(D_TILES):
                 weighted_sums(3, k, dt, "turn_bank" if k else "sum_bank")
         for k in range(K_TILES):
             for dt in range(D_TILES):
                 subtract_centres(3, k, dt)
-                when(k + dt == 0, normalise, 2, 1, False)
                 when(k + dt == 2, add_eps, 3, 0)
                 sum_squares(3, k, dt)
         normalise(3, 0, True)

@@ -26,7 +26,7 @@ HALVES = N // PASS
 E_PASSES = E // PASS
 K_TILES = K // P
 D_TILES = D // PASS
-RUN = 4
+RUN = 2
 X_AHEAD = 5
 PIECE = D // PACK
 XN = (3, 3, 3, 3, 3, 3, 3, 3)

from contextlib import ExitStack

import concourse.mybir as mybir
from concourse.masks import make_identity

B, N, E, K, D = 4, 1024, 1024, 256, 1024
EPS = 1e-5
FLOPS = 2 * B * N * E * K + 2 * B * N * K * D

F32 = mybir.dt.float32
BF16 = mybir.dt.bfloat16
U32 = mybir.dt.uint32
I32 = mybir.dt.int32
U8 = mybir.dt.uint8
FP8 = mybir.dt.float8_e4m3fn
FP8X4 = mybir.dt.float8_e4m3fn_x4
ALU = mybir.AluOpType
ACT = mybir.ActivationFunctionType
AXIS = mybir.AxisListType

P = 128
PACK = 4
PASS = P * PACK
GROUPS = B * N // PASS
HALVES = N // PASS
E_PASSES = E // PASS
K_TILES = K // P
D_TILES = D // PASS
RUN = 2
X_AHEAD = 5
PIECE = D // PACK
XN = (3, 3, 3, 3, 3, 3, 3, 3)
SV = (7,)


def tile_crossmodalreweightedvlad_w8_kernel(tc, y_bytes, y_scale, w_words, w_scales, b, t, x, c, out):
    nc = tc.nc
    with ExitStack() as ctx:
        const = ctx.enter_context(tc.tile_pool(name="const", bufs=1))
        work = ctx.enter_context(tc.tile_pool(name="work", bufs=2))
        psum = ctx.enter_context(tc.psum_pool(name="psum", bufs=2))
        ctx.enter_context(tc.manual_schedule())

        y_raw, x_raw, y_scaled, y_banks, y_grouped, y_codes, y_planes = {}, {}, {}, {}, {}, {}, {}
        logit_banks, z_by_cluster, z_banks, neg_max, expo, row_sum, inv_sum, coef = {}, {}, {}, {}, {}, {}, {}, {}
        x_banks = {}
        r_grouped, r_codes, r_planes, x_grouped, x_codes, x_planes = {}, {}, {}, {}, {}, {}
        mass_banks, mass_rows, neg_mass, sum_banks, resid, squares, mean_sq, rstd, result = {}, {}, {}, {}, {}, {}, {}, {}, {}

        def rows_of(tensor, g):
            return tensor[g // HALVES, (g % HALVES) * PASS : (g % HALVES + 1) * PASS, :].rearrange("(p j) f -> p j f", j=PACK)

        def load_y(g):
            y_raw[g] = work.tile([P, PACK, E], U8, name="y_raw", bufs=GROUPS)
            nc.sync.dma_start(out=y_raw[g][:], in_=rows_of(y_bytes, g))

        def load_x(g, half):
            x_raw[g, half] = work.tile([P, PACK, PASS], BF16, name="x_raw", bufs=2 * X_AHEAD)
            nc.sync.dma_start(out=x_raw[g, half][:], in_=rows_of(x, g)[:, :, half * PASS : (half + 1) * PASS])

        ident = const.tile([P, P], F32, name="ident")
        make_identity(nc, ident[:])
        minus_half = const.tile([P, 1], F32, name="minus_half")
        nc.gpsimd.memset(minus_half[:], -0.5)
        ident_bf16 = const.tile([P, P], BF16, name="ident_bf16")
        make_identity(nc, ident_bf16[:])
        w_plane = const.tile([P, E_PASSES, K], U8, name="w_plane", align_bytes=64)
        nc.vector.memset(w_plane[:].bitcast(I32), 0)
        warm = const.tile([P, 1], F32, name="warm")
        nc.scalar.activation(out=warm[:], in_=minus_half[:], func=ACT.Exp)

        scale_cols = const.tile([P, E // P], F32, name="scale_cols")
        nc.sync.dma_start(out=scale_cols[:], in_=y_scale.rearrange("o u (p j) -> p (o u j)", p=P))
        load_x(0, 0)
        load_y(0)
        load_x(0, 1)
        load_x(1, 0)
        load_y(1)
        w_code = const.tile([P, E_PASSES, K], U32, name="w_code", align_bytes=64)
        nc.sync.dma_start(out=w_code[:].bitcast(I32), in_=w_words.rearrange("g p n j -> p g (n j)").bitcast(I32))
        for quad in range(4):
            nc.sync.dma_start(
                out=w_plane[32 * quad : 32 * quad + 4, :, :].bitcast(I32),
                in_=w_scales[:, 4 * quad : 4 * quad + 4, :].rearrange("g q n -> q g n").bitcast(I32),
            )
        bias_raw = const.tile([P, K_TILES, 2], BF16, name="bias_raw")
        with nc.allow_non_contiguous_dma(reason="one bias value for each partition"):
            nc.sync.dma_start(out=bias_raw[:, :, 0:1], in_=b.rearrange("(k p o) -> p k o", p=P, o=1))
        load_x(1, 1)
        t_cols = const.tile([P, HALVES, PACK], BF16, name="t_cols")
        nc.sync.dma_start(out=t_cols[:], in_=t.rearrange("(h p j) -> p h j", p=P, j=PACK))
        for g in range(2, X_AHEAD):
            load_y(g)
            load_x(g, 0)
            load_x(g, 1)
        centres = const.tile([P, K_TILES, D], BF16, name="centres")
        nc.sync.dma_start(out=centres[:], in_=c.rearrange("(k p) d -> p k d", p=P))
        for g in range(X_AHEAD, GROUPS):
            load_y(g)

        scale_rows = const.tile([P, P, E // P], F32, name="scale_rows")

        def spread_scale(half):
            bank = psum.tile([P, PACK, P], F32, name="turn_bank")
            for j in range(PACK):
                col = half * PACK + j
                nc.tensor.transpose(bank[:, j, :], scale_cols[:, col : col + 1].to_broadcast([P, P]), ident[:])
            nc.vector.tensor_copy(out=scale_rows[:, :, half * PACK : (half + 1) * PACK], in_=bank[:].rearrange("q j n -> q n j"))

        def scale_y(g, j):
            y_scaled[g, j] = work.tile([P, E], BF16, name="y_scaled", bufs=4)
            nc.vector.tensor_tensor(
                out=y_scaled[g, j][:], in0=y_raw[g][:, j, :].bitcast(FP8), in1=scale_rows[:].rearrange("q n j -> q (n j)"), op=ALU.mult
            )

        def turn_y(g, j):
            words = y_scaled[g, j][:].bitcast(F32)
            y_banks[g, j] = psum.tile([P, E_PASSES, 2, P], F32, name="turn_bank")
            for a in range(E_PASSES):
                for u in range(2):
                    nc.tensor.transpose(y_banks[g, j][:, a, u, :], words[:, 2 * P * a + u : 2 * P * (a + 1) : 2], ident[:])

        def group_y(g, j):
            if j == 0:
                y_grouped[g] = work.tile([P, E_PASSES, PACK, P, 2], F32, name="y_grouped", align_bytes=64)
            nc.scalar.copy(out=y_grouped[g][:, :, j, :, :], in_=y_banks[g, j][:].rearrange("q a u p -> q a p u"))

        def quantize_y(g):
            y_codes[g] = work.tile([P, E_PASSES * PASS], U32, name="y_codes", align_bytes=64)
            y_planes[g] = work.tile([P, E_PASSES * PASS], U8, name="y_planes", align_bytes=64)
            nc.vector.quantize_mx(
                out=y_codes[g][:].bitcast(FP8X4),
                scales=y_planes[g][:],
                in_=y_grouped[g][:].rearrange("q a j p u -> q (a j p u)").bitcast(BF16),
            )

        def logits(g, k):
            logit_banks[g, k] = psum.tile([P, PASS], F32, name="logit_bank", bufs=1)
            for a in range(E_PASSES):
                nc.tensor.matmul_mx(
                    out=logit_banks[g, k][:],
                    lhsT=w_code[:, a, k * P : (k + 1) * P].bitcast(FP8X4),
                    lhsT_scale=w_plane[:, a, k * P : (k + 1) * P],
                    rhs=y_codes[g][:, a * PASS : (a + 1) * PASS].bitcast(FP8X4),
                    rhs_scale=y_planes[g][:, a * PASS : (a + 1) * PASS],
                    start=(a == 0),
                    stop=(a == E_PASSES - 1),
                )

        def add_bias(g, k):
            z_by_cluster[g, k] = work.tile([P, PASS], F32, name="z_by_cluster", bufs=3)
            nc.scalar.activation(
                out=z_by_cluster[g, k][:], in_=logit_banks[g, k][:], func=ACT.Identity, bias=bias_raw[:, k, 0:1]
            )

        def turn_z(g, pair):
            z_banks[g, pair] = psum.tile([P, 2, K], F32, name="z_bank")
            for jj in range(2):
                j = 2 * pair + jj
                for k in range(K_TILES):
                    nc.tensor.transpose(z_banks[g, pair][:, jj, k * P : (k + 1) * P], z_by_cluster[g, k][:, j * P : (j + 1) * P], ident[:])

        def find_max(g, pair):
            neg_max[g, pair] = work.tile([P, 2], F32, name="neg_max", bufs=4)
            nc.vector.tensor_reduce(out=neg_max[g, pair][:], in_=z_banks[g, pair][:], axis=AXIS.X, op=ALU.max, negate=True)

        def exponentiate(g, j):
            if j == 0:
                expo[g] = work.tile([P, PACK, K], F32, name="expo", bufs=3)
                row_sum[g] = work.tile([P, PACK], F32, name="row_sum")
            nc.scalar.activation(
                out=expo[g][:, j, :],
                in_=z_banks[g, j // 2][:, j % 2, :],
                func=ACT.Exp,
                bias=neg_max[g, j // 2][:, j % 2 : j % 2 + 1],
                accum_out=row_sum[g][:, j : j + 1],
            )

        def invert_sum(g):
            inv_sum[g] = work.tile([P, PACK], F32, name="inv_sum")
            nc.vector.reciprocal(out=inv_sum[g][:], in_=row_sum[g][:])

        def make_coef(g):
            coef[g] = work.tile([P, PACK], F32, name="coef")
            nc.vector.tensor_tensor(out=coef[g][:], in0=inv_sum[g][:], in1=t_cols[:, g % HALVES, :], op=ALU.mult)

        def reweight(g):
            r_grouped[g] = work.tile([P, K, PACK], BF16, name="r_grouped", align_bytes=64)
            nc.vector.tensor_tensor(
                out=r_grouped[g][:].rearrange("p (c i) j -> p c j i", i=2),
                in0=expo[g][:].rearrange("p j (c i) -> p c j i", i=2),
                in1=coef[g][:].unsqueeze(1).unsqueeze(3).to_broadcast([P, K // 2, PACK, 2]),
                op=ALU.mult,
            )

        def quantize_r(g):
            r_codes[g] = work.tile([P, K], U32, name="r_codes", bufs=6, align_bytes=64)
            r_planes[g] = work.tile([P, K], U8, name="r_planes", bufs=6, align_bytes=64)
            nc.vector.quantize_mx(
                out=r_codes[g][:].bitcast(FP8X4), scales=r_planes[g][:], in_=r_grouped[g][:].rearrange("p k j -> p (k j)")
            )

        def add_mass(g, j):
            i = g // HALVES
            first = g % HALVES == 0 and j == 0
            if first:
                mass_banks[i] = psum.tile([P, 2, K], F32, name="mass_bank", bufs=1)
            nc.tensor.matmul(
                out=mass_banks[i][:, 0, :],
                lhsT=inv_sum[g][:, j : j + 1].to_broadcast([P, P]),
                rhs=expo[g][:, j, :],
                start=first,
                stop=(g % HALVES == HALVES - 1 and j == PACK - 1),
            )

        def copy_mass(i):
            mass_rows[i] = work.tile([P, K], F32, name="mass_rows")
            nc.scalar.copy(out=mass_rows[i][:], in_=mass_banks[i][:, 0, :])

        def turn_mass(i):
            for k in range(K_TILES):
                nc.tensor.transpose(mass_banks[i][:, 1, k * P : (k + 1) * P], mass_rows[i][:, k * P : (k + 1) * P], ident[:])

        def negate_mass(i):
            neg_mass[i] = work.tile([P, K_TILES], F32, name="neg_mass", bufs=4)
            nc.scalar.activation(out=neg_mass[i][:], in_=mass_banks[i][:, 1, 0:K:P], func=ACT.Copy, scale=-1.0)

        def group_x(g, piece):
            if piece == 0:
                x_grouped[g] = work.tile([P, D, PACK], BF16, name="x_grouped", bufs=3, align_bytes=64)
            src = x_raw[g, piece // 2][:, :, (piece % 2) * PIECE : (piece % 2 + 1) * PIECE].rearrange("p j (c i) -> p c j i", i=RUN)
            dst = x_grouped[g][:, piece * PIECE : (piece + 1) * PIECE, :].rearrange("p (c i) j -> p c j i", i=RUN)
            nc.scalar.copy(out=dst, in_=src)
            if piece % 2 == 1 and g + X_AHEAD < GROUPS:
                load_x(g + X_AHEAD, piece // 2)

        def weave_x(g, piece):
            x_banks[g, piece] = psum.tile([P, 2, PASS], BF16, name="turn_bank")
            for half in range(2):
                first = (piece % 2) * PIECE + half * P
                nc.tensor.matmul(
                    out=x_banks[g, piece][:, half, :],
                    lhsT=ident_bf16[:],
                    rhs=x_raw[g, piece // 2][:, :, first : first + P].rearrange("p j d -> p d j"),
                    start=True,
                    stop=True,
                )

        def copy_woven_x(g, piece):
            if piece == 0:
                x_grouped[g] = work.tile([P, D, PACK], BF16, name="x_grouped", bufs=3, align_bytes=64)
            nc.scalar.copy(
                out=x_grouped[g][:, piece * PIECE : (piece + 1) * PIECE, :].rearrange("p d j -> p (d j)"),
                in_=x_banks[g, piece][:].rearrange("p h n -> p (h n)"),
            )

        def quantize_x(g):
            x_codes[g] = work.tile([P, D], U32, name="x_codes", bufs=5, align_bytes=64)
            x_planes[g] = work.tile([P, D], U8, name="x_planes", bufs=5, align_bytes=64)
            nc.vector.quantize_mx(
                out=x_codes[g][:].bitcast(FP8X4), scales=x_planes[g][:], in_=x_grouped[g][:].rearrange("p d j -> p (d j)")
            )

        def weighted_sums(i, k, dt, bank_name="sum_bank"):
            sum_banks[i, k, dt] = psum.tile([P, PASS], F32, name=bank_name)
            for h in range(HALVES):
                g = i * HALVES + h
                nc.tensor.matmul_mx(
                    out=sum_banks[i, k, dt][:],
                    lhsT=r_codes[g][:, k * P : (k + 1) * P].bitcast(FP8X4),
                    lhsT_scale=r_planes[g][:, k * P : (k + 1) * P],
                    rhs=x_codes[g][:, dt * PASS : (dt + 1) * PASS].bitcast(FP8X4),
                    rhs_scale=x_planes[g][:, dt * PASS : (dt + 1) * PASS],
                    start=(h == 0),
                    stop=(h == HALVES - 1),
                )

        def subtract_centres(i, k, dt):
            if dt == 0:
                resid[i, k] = work.tile([P, D], F32, name="resid", bufs=4)
            cols = slice(dt * PASS, (dt + 1) * PASS)
            nc.vector.scalar_tensor_tensor(
                out=resid[i, k][:, cols],
                in0=centres[:, k, cols],
                scalar=neg_mass[i][:, k : k + 1],
                in1=sum_banks[i, k, dt][:],
                op0=ALU.mult,
                op1=ALU.add,
            )

        def sum_squares(i, k, dt):
            if dt == 0:
                squares[i, k] = work.tile([P, D_TILES], F32, name="squares", bufs=4)
                result[i, k] = work.tile([P, D], F32, name="result", bufs=4)
            cols = slice(dt * PASS, (dt + 1) * PASS)
            nc.scalar.activation(
                out=result[i, k][:, cols],
                in_=resid[i, k][:, cols],
                func=ACT.Square,
                scale=D**-0.5,
                accum_out=squares[i, k][:, dt : dt + 1],
            )

        def add_eps(i, k):
            mean_sq[i, k] = work.tile([P, 1], F32, name="mean_sq", bufs=4)
            nc.vector.tensor_scalar(
                out=mean_sq[i, k][:], in0=squares[i, k][:, 0:1], scalar1=squares[i, k][:, 1:2], scalar2=EPS, op0=ALU.add, op1=ALU.add
            )
            rstd[i, k] = work.tile([P, 1], F32, name="rstd", bufs=4)
            nc.gpsimd.tensor_tensor(out=rstd[i, k][:], in0=mean_sq[i, k][:], in1=minus_half[:], op=ALU.pow)

        def normalise(i, k, on_vector, cols=slice(0, D)):
            if on_vector:
                nc.vector.tensor_scalar(out=result[i, k][:, cols], in0=resid[i, k][:, cols], scalar1=rstd[i, k][:], scalar2=None, op0=ALU.mult)
            else:
                nc.scalar.activation(out=result[i, k][:, cols], in_=resid[i, k][:, cols], func=ACT.Copy, scale=rstd[i, k][:])
            nc.sync.dma_start(out=out[i, k * P : (k + 1) * P, cols], in_=result[i, k][:, cols])

        def when(ok, stage, *args):
            if ok:
                stage(*args)

        group_x(0, 0)
        spread_scale(0)
        spread_scale(1)
        scale_y(0, 0)
        turn_y(0, 0)
        for piece in range(1, PACK):
            group_x(0, piece)

        pieces = [(g, piece) for g in range(1, GROUPS) for piece in range(PACK)]
        slots = [(step, q) for step in range(GROUPS) for q in range(XN[step])]
        x_slot = dict(zip(slots, pieces))
        x_ready = {step + (q > 0): g for (step, q), (g, piece) in x_slot.items() if piece == PACK - 1}
        x_ready[0] = 0

        def x_piece(step, q):
            if (step, q) in x_slot:
                group_x(*x_slot[step, q])

        for step in range(GROUPS):
            ga, gb, gc, gd = step, step - 1, step - 2, step - 3
            n_on, b_on, c_on, d_on = step + 1 < GROUPS, gb >= 0, gc >= 0, gd >= 0
            ip, kp = divmod(step - 4, K_TILES)
            p_on = ip >= 0
            io, ko = divmod(step - 5, K_TILES)
            o_on = io >= 0
            m_on = d_on and gd % HALVES == HALVES - 1

            scale_y(ga, 1)
            when(c_on, find_max, gc, 0)
            when(d_on, quantize_r, gd)
            when(c_on, find_max, gc, 1)
            when(d_on, add_mass, gd, 2)
            when(d_on, add_mass, gd, 3)
            turn_y(ga, 1)
            group_y(ga, 0)
            when(o_on, sum_squares, io, ko, 1)
            x_piece(step, 0)
            when(m_on, copy_mass, gd // HALVES)

            when(b_on, quantize_y, gb)
            scale_y(ga, 2)
            when(p_on, weighted_sums, ip, kp, 0)
            when(m_on, turn_mass, gd // HALVES)
            when(b_on, logits, gb, 0)
            turn_y(ga, 2)
            for j in range(PACK):
                when(c_on, exponentiate, gc, j)
            when(m_on, negate_mass, gd // HALVES)
            group_y(ga, 1)
            when(b_on, add_bias, gb, 0)

            scale_y(ga, 3)
            when(o_on, add_eps, io, ko)
            when(p_on, subtract_centres, ip, kp, 0)
            when(c_on, invert_sum, gc)
            when(step in x_ready, quantize_x, x_ready.get(step))
            when(p_on, weighted_sums, ip, kp, 1)
            when(b_on, logits, gb, 1)
            turn_y(ga, 3)
            x_piece(step, 1)
            when(b_on, add_bias, gb, 1)
            group_y(ga, 2)

            when(c_on, make_coef, gc)
            when(n_on, scale_y, ga + 1, 0)
            when(c_on, reweight, gc)
            when(p_on, subtract_centres, ip, kp, 1)
            when(o_on and step in SV, normalise, io, ko, True)
            when(c_on, add_mass, gc, 0)
            when(b_on, turn_z, gb, 0)
            when(b_on, turn_z, gb, 1)
            when(c_on, add_mass, gc, 1)
            group_y(ga, 3)
            when(n_on, turn_y, ga + 1, 0)
            when(not n_on, weave_x, ga, 0)
            when(p_on, sum_squares, ip, kp, 0)
            x_piece(step, 2)
            when(o_on and step not in SV, normalise, io, ko, False)

        quantize_y(7)
        sum_squares(1, 1, 1)
        add_eps(1, 1)
        find_max(6, 0)
        find_max(6, 1)
        quantize_r(5)
        quantize_x(6)
        normalise(1, 1, True)
        add_mass(5, 2)
        add_mass(5, 3)
        weave_x(7, 1)
        copy_woven_x(7, 0)
        copy_mass(2)
        logits(7, 0)
        copy_woven_x(7, 1)
        add_bias(7, 0)
        turn_mass(2)
        weave_x(7, 2)
        logits(7, 1)
        weighted_sums(2, 0, 0)
        weighted_sums(2, 0, 1)
        for j in range(PACK):
            exponentiate(6, j)
        negate_mass(2)
        weave_x(7, 3)
        add_bias(7, 1)
        copy_woven_x(7, 2)
        invert_sum(6)
        subtract_centres(2, 0, 0)
        make_coef(6)
        subtract_centres(2, 0, 1)
        turn_z(7, 0)
        turn_z(7, 1)
        weighted_sums(2, 1, 0)
        weighted_sums(2, 1, 1)
        for j in range(PACK):
            add_mass(6, j)
        sum_squares(2, 0, 0)
        sum_squares(2, 0, 1)
        find_max(7, 0)
        find_max(7, 1)
        for j in range(PACK):
            exponentiate(7, j)
        copy_woven_x(7, 3)
        add_eps(2, 0)
        subtract_centres(2, 1, 0)
        subtract_centres(2, 1, 1)
        invert_sum(7)
        reweight(6)
        make_coef(7)
        for j in range(PACK):
            add_mass(7, j)
        sum_squares(2, 1, 0)
        sum_squares(2, 1, 1)
        normalise(2, 0, False)
        quantize_x(7)
        quantize_r(6)
        reweight(7)
        add_eps(2, 1)
        quantize_r(7)
        copy_mass(3)
        turn_mass(3)
        negate_mass(3)
        normalise(2, 1, True)
        for k in range(K_TILES):
            for dt in range(D_TILES):
                weighted_sums(3, k, dt, "turn_bank" if k else "sum_bank")
        for k in range(K_TILES):
            for dt in range(D_TILES):
                subtract_centres(3, k, dt)
                when(k + dt == 2, add_eps, 3, 0)
                sum_squares(3, k, dt)
        normalise(3, 0, True)
        add_eps(3, 1)
        for dt in range(D_TILES):
            normalise(3, 1, True, slice(dt * PASS, (dt + 1) * PASS))
